import numpy as np
import ml_dtypes


def mxq(x, axis, fmt="e4m3"):
    dtype, down = {"e4m3": (ml_dtypes.float8_e4m3fn, 7), "e5m2": (ml_dtypes.float8_e5m2, 14)}[fmt]
    v = np.moveaxis(np.asarray(x, np.float32).astype(ml_dtypes.bfloat16).astype(np.float64), axis, -1)
    blocks = v.reshape(v.shape[:-1] + (-1, 32))
    amax = np.abs(blocks).max(-1, keepdims=True)
    byte = np.maximum(np.where(amax > 0, np.frexp(amax)[1] - 1 + 127, 0) - down, 1)
    scale = np.exp2(byte - 127.0)
    codes = (blocks / scale).astype(np.float32).astype(dtype).astype(np.float64)
    return np.moveaxis((codes * scale).reshape(v.shape), -1, axis)


WIDE = False


def mx_kscale(k):
    if not WIDE:
        return np.ones(k)
    levels = np.array([10, -10, 5, -5, 0])
    if k % 512:
        return np.exp2(np.random.permutation(np.resize(levels, k // 32))).repeat(32)
    a = np.empty((k // 512, 16))
    for p in range(k // 512):
        a[p, :8] = np.random.permutation(np.resize(levels, 8))
        for g in range(8):
            far = levels[np.abs(levels - a[p, g]) >= 10]
            a[p, g + 8] = far[np.random.randint(len(far))]
    return np.exp2(a.ravel()).repeat(32)


def f64(x):
    return np.asarray(x).astype(np.float64)


def striped(idx):
    return np.tile(np.asarray(idx).reshape(-1, 16).T, (8, 1)).astype(np.uint16)


def unstriped(offs):
    return offs[:16].T.reshape(-1).astype(np.int64)


E2M1 = np.array([0.0, 0.5, 1.0, 1.5, 2.0, 3.0, 4.0, 6.0, -0.0, -0.5, -1.0, -1.5, -2.0, -3.0, -4.0, -6.0])


def pack_weight(w, fmt):
    k, n = w.shape
    w = f64(np.asarray(w, np.float32).astype(ml_dtypes.bfloat16)).reshape(k // 32, 32, n)
    amax = np.abs(w).max(1)
    if fmt == "e4m3":
        byte = np.frexp(amax)[1] - 1 + 127 - 7
    else:
        mant, ex = np.frexp(amax / 6.0)
        byte = np.where(mant > 0.5, ex, ex - 1) + 127
    byte = np.clip(np.where(amax > 0, byte, 1), 1, 254)
    scaled = (w * np.exp2(127.0 - byte)[:, None, :]).reshape(k, n).astype(np.float32)
    by_word = np.ascontiguousarray(scaled.reshape(k // 512, 128, 4, n).transpose(0, 1, 3, 2))
    if fmt == "e4m3":
        words = by_word.astype(ml_dtypes.float8_e4m3fn).view(np.uint8)
    else:
        c = by_word.astype(ml_dtypes.float4_e2m1fn).view(np.uint8) & 0xF
        words = (c[..., 0::2] | (c[..., 1::2] << 4)).reshape(k // 512, 128, 2 * n)
    return np.ascontiguousarray(words), np.ascontiguousarray(byte.astype(np.uint8).reshape(k // 512, 16, n))


def unpack_weight(words, scales, fmt):
    g, _, n = scales.shape
    words = np.ascontiguousarray(words).reshape(g, 128, n, -1)
    if fmt == "e4m3":
        vals = words.view(ml_dtypes.float8_e4m3fn).astype(np.float64)
    else:
        nib = np.empty((g, 128, n, 4), np.uint8)
        nib[..., 0::2] = words & 0xF
        nib[..., 1::2] = words >> 4
        vals = E2M1[nib]
    vals = vals * np.repeat(np.exp2(scales.astype(np.float64) - 127.0), 8, axis=1)[..., None]
    return vals.transpose(0, 1, 3, 2).reshape(g * 512, n)


D, E, T, I, Q = 512, 512, 1024, 256, 512


def setup_inputs():
    n = np.random.standard_normal
    idx = np.random.permutation(T)[:I]
    fd = mx_kscale(D)
    fq = mx_kscale(Q)
    keysp = pack_weight(n((D, T)) / fd[:, None], "e4m3")
    return {
        "query": (n((D, Q)) * 0.9 / np.sqrt(D) * fd[:, None]).astype(np.float32),
        "query2": (n((D, Q)) * 0.6 / np.sqrt(D) * fd[:, None]).astype(np.float32),
        "keys_words": keysp[0],
        "keys_scales": keysp[1],
        "size": (np.random.uniform(0.5, 2.0, (1, I))).astype(np.float32),
        "qs": (np.random.uniform(2.0, 8.0, (Q, 1)) * fq[:, None]).astype(np.float32),
        "grows": (n((Q, E)) / fq[:, None]).astype(np.float32),
        "old": (n((E, T)) * 2.0).astype(np.float32),
        "fade": (np.random.uniform(0.5, 1.0, (1, T))).astype(np.float32),
        "offs": striped(idx),
    }


def reference(query, query2, keys_words, keys_scales, size, qs, grows, old, fade, offs):
    idx = unstriped(offs)
    keysu = unpack_weight(keys_words, keys_scales, "e4m3")
    queryq = mxq(f64(query), 0, "e4m3")
    keysidxg = keysu[:, idx]
    a = queryq.T @ keysidxg
    query2q = mxq(f64(query2), 0, "e4m3")
    b = query2q.T @ keysidxg
    pa = np.exp(a - np.max(a, axis=1, keepdims=True))
    wa = pa / np.sum(pa, axis=1, keepdims=True)
    pb = np.exp(b - np.max(b, axis=1, keepdims=True))
    wb = pb / np.sum(pb, axis=1, keepdims=True)
    w = wa * wb / (wa + wb) * f64(size)
    wq = w * f64(qs)
    growsq = mxq(f64(grows), 0, "e4m3")
    wqq = mxq(wq, 0, "e4m3")
    gv = growsq.T @ wqq
    gf = np.zeros((E, T))
    gf[:, idx] = gv
    y = f64(old) * f64(fade) + gf
    return y

@@ -1,0 +1,243 @@
+from contextlib import ExitStack
+
+import concourse.mybir as mybir
+from concourse.masks import make_identity
+
+D, E, T, I, Q = 512, 512, 1024, 256, 512
+FLOPS = 2 * (2 * D * Q * I + Q * E * I)
+
+F32 = mybir.dt.float32
+BF16 = mybir.dt.bfloat16
+I32 = mybir.dt.int32
+U32 = mybir.dt.uint32
+U16 = mybir.dt.uint16
+U8 = mybir.dt.uint8
+FP8X4 = mybir.dt.float8_e4m3fn_x4
+ALU = mybir.AluOpType
+ACT = mybir.ActivationFunctionType
+AXIS_X = mybir.AxisListType.X
+
+P = 128
+PACK = 4
+BANK = 512
+
+
+def tile_attend_bagreement_v_kernel(
+    tc, query, query2, keys_words, keys_scales, size, qs, grows, old, fade, offs, out
+):
+    nc = tc.nc
+    with ExitStack() as ctx:
+        sb = ctx.enter_context(tc.tile_pool(name="sb", bufs=1))
+        ps = ctx.enter_context(tc.psum_pool(name="ps", bufs=1))
+
+        offsets = sb.tile([P, I // 16], U16, name="offsets")
+        nc.sync.dma_start(offsets[:], offs)
+
+        key_bytes = sb.tile([P, T], U8, name="key_bytes", align_bytes=64)
+        nc.gpsimd.memset(key_bytes[:].bitcast(I32), 0)
+        for quad in range(4):
+            nc.scalar.dma_start(
+                key_bytes[32 * quad : 32 * quad + 4, :].bitcast(I32),
+                keys_scales[0, 4 * quad : 4 * quad + 4, :].bitcast(I32),
+            )
+
+        fade_col = sb.tile([P, 2, 4], F32, name="fade_col")
+        nc.scalar.dma_start(fade_col[:], fade.rearrange("o (h p m) -> p (o h) m", h=2, m=4))
+        size_col = sb.tile([P, 2], F32, name="size_col")
+        nc.scalar.dma_start(size_col[:], size.rearrange("o (p m) -> p (o m)", m=2))
+        qs_sb = sb.tile([P, PACK], F32, name="qs_sb")
+        nc.scalar.dma_start(qs_sb[:], qs.rearrange("(p r) o -> p (r o)", r=PACK))
+
+        def load_rows(src, name):
+            raw = sb.tile([P, PACK, 512], F32, name=name)
+            nc.sync.dma_start(raw[:], src.rearrange("(p j) c -> p j c", j=PACK))
+            return raw
+
+        qa_raw = load_rows(query, "qa_raw")
+        key_words = sb.tile([P, T], I32, name="key_words", align_bytes=64)
+        nc.sync.dma_start(key_words[:], keys_words[0].rearrange("p n t -> p (n t)").bitcast(I32))
+        qb_raw = load_rows(query2, "qb_raw")
+        grows_raw = load_rows(grows, "grows_raw")
+        old_sb = []
+        for c in range(4):
+            t = sb.tile([P, T], F32, name=f"old{c}")
+            nc.sync.dma_start(t[:], old[c * P : (c + 1) * P, :])
+            old_sb.append(t)
+
+        ident = sb.tile([P, P], F32, name="ident")
+        make_identity(nc, ident[:])
+
+        placed = []
+        for c in range(4):
+            t = sb.tile([P, T], F32, name=f"placed{c}")
+            nc.vector.memset(t[:], 0.0)
+            placed.append(t)
+
+        fade_ps = []
+        fade_sb = sb.tile([P, T], F32, name="fade_sb")
+        for h in range(2):
+            bank = ps.tile([P, 4, P], F32, name=f"fade_ps{h}")
+            for m in range(4):
+                nc.tensor.transpose(bank[:, m, :], fade_col[:, h, m : m + 1].to_broadcast([P, P]), ident[:])
+            view = bank[:].rearrange("p m n -> p n m")
+            fade_ps.append(view)
+            nc.scalar.copy(fade_sb[:, h * BANK : (h + 1) * BANK].rearrange("p (n m) -> p n m", m=4), view)
+        size_bank = ps.tile([P, 2, P], F32, name="size_ps")
+        for m in range(2):
+            nc.tensor.transpose(size_bank[:, m, :], size_col[:, m : m + 1].to_broadcast([P, P]), ident[:])
+        size_ps = size_bank[:].rearrange("p m n -> p n m")
+
+        key_scale = sb.tile([P, I], U8, name="key_scale", align_bytes=64)
+        nc.vector.tensor_copy(key_scale[:], key_bytes[:].indirect(offsets[:]))
+
+        def quantize(grouped, width, name):
+            codes = sb.tile([P, width], U32, name=name + "_codes", align_bytes=64)
+            scales = sb.tile([P, width], U8, name=name + "_scales", align_bytes=64)
+            nc.vector.quantize_mx(out=codes[:].bitcast(FP8X4), scales=scales[:], in_=grouped)
+            return codes, scales
+
+        def deal(raw, half, name, on_vector):
+            grouped = sb.tile([P, 2 * P * PACK], BF16, name=name, align_bytes=64)
+            dst = grouped[:].rearrange("p (r s j) -> p s j r", r=2, j=PACK)
+            src = raw[:].rearrange("p j (s r) -> p s j r", r=PACK)[:, :, :, 2 * half : 2 * half + 2]
+            if on_vector:
+                nc.vector.tensor_copy(dst, src)
+            else:
+                nc.scalar.copy(dst, src)
+            return grouped
+
+        key_codes = sb.tile([P, I], U32, name="key_codes", align_bytes=64)
+
+        def scores(grouped, half, name):
+            codes, scales = quantize(grouped[:], 2 * P, f"{name}{half}")
+            bank = ps.tile([P, 2, I], F32, name=f"{name}_ps{half}", tag=f"{name}_ps{half}")
+            for k in range(2):
+                cols = slice(k * P, (k + 1) * P)
+                nc.tensor.matmul_mx(
+                    out=bank[:, k, :],
+                    lhsT=codes[:, cols].bitcast(FP8X4),
+                    lhsT_scale=scales[:, cols],
+                    rhs=key_codes[:].bitcast(FP8X4),
+                    rhs_scale=key_scale[:],
+                    start=True,
+                    stop=True,
+                )
+            return bank
+
+        def row_max(bank, name):
+            neg = sb.tile([P, 2], F32, name=name + "_neg")
+            pos = sb.tile([P, 2], F32, name=name + "_pos")
+            nc.vector.tensor_reduce(out=neg[:], in_=bank[:], axis=AXIS_X, op=ALU.max, negate=True)
+            nc.vector.tensor_scalar(pos[:], neg[:], -1.0, None, ALU.mult)
+            return neg, pos
+
+        def exps(bank, neg, pos, name):
+            total = sb.tile([P, 2], F32, name=name + "_sum")
+            inv = sb.tile([P, 2, I], F32, name=name + "_inv")
+            unread = sb.tile([P, 2, I], F32, name=name + "_unread")
+            for k in range(2):
+                nc.scalar.activation(
+                    unread[:, k, :], bank[:, k, :], ACT.Exp, bias=neg[:, k : k + 1], scale=1.0,
+                    accum_out=total[:, k : k + 1],
+                )
+            for k in range(2):
+                nc.scalar.activation(inv[:, k, :], bank[:, k, :], ACT.Exp, bias=pos[:, k : k + 1], scale=-1.0)
+            return total, inv
+
+        ga = [deal(qa_raw, half, f"ga{half}", half == 0) for half in range(2)]
+        nc.vector.tensor_copy(key_codes[:], key_words[:].bitcast(U32).indirect(offsets[:]))
+        a_banks = [scores(ga[half], half, "a") for half in range(2)]
+        a_max = [row_max(a_banks[half], f"amax{half}") for half in range(2)]
+        a_exp = [exps(a_banks[half], *a_max[half], f"aexp{half}") for half in range(2)]
+        b_banks = []
+        b_exp = []
+        for half in range(2):
+            bank = scores(deal(qb_raw, half, f"gb{half}", True), half, "b")
+            neg, pos = row_max(bank, f"bmax{half}")
+            b_exp.append(exps(bank, neg, pos, f"bexp{half}"))
+
+        inv_sum_a = []
+        factor = []
+        for half in range(2):
+            inv = sb.tile([P, 2], F32, name=f"inv_sum_a{half}")
+            nc.vector.reciprocal(inv[:], a_exp[half][0][:])
+            fac = sb.tile([P, 2], F32, name=f"factor{half}")
+            nc.vector.tensor_tensor(fac[:], inv[:], qs_sb[:, 2 * half : 2 * half + 2], ALU.mult)
+            inv_sum_a.append(inv)
+            factor.append(fac)
+
+
+        dens = []
+        for half in range(2):
+            ratio = sb.tile([P, 2], F32, name=f"ratio{half}")
+            nc.vector.tensor_tensor(ratio[:], b_exp[half][0][:], inv_sum_a[half][:], ALU.mult)
+            den = sb.tile([P, 2, I], F32, name=f"den{half}")
+            for k in range(2):
+                nc.vector.scalar_tensor_tensor(
+                    den[:, k, :], b_exp[half][1][:, k, :], ratio[:, k : k + 1], a_exp[half][1][:, k, :],
+                    ALU.mult, ALU.add,
+                )
+            dens.append(den)
+
+        grows_q = []
+        for half in range(2):
+            grouped = sb.tile([P, 2 * P * PACK], BF16, name=f"grows_grouped{half}", align_bytes=64)
+            nc.vector.tensor_copy(
+                grouped[:].rearrange("p (c i j) -> p c j i", i=4, j=PACK),
+                grows_raw[:, :, half * 2 * P : (half + 1) * 2 * P].rearrange("p j (c i) -> p c j i", i=4),
+            )
+            grows_q.append(quantize(grouped[:], 2 * P, f"grows{half}"))
+
+        faded = [sb.tile([P, T], F32, name=f"faded{c}") for c in range(4)]
+        for c in range(2):
+            for h in range(2):
+                cols = slice(h * BANK, (h + 1) * BANK)
+                nc.vector.tensor_tensor(
+                    faded[c][:, cols].rearrange("p (n m) -> p n m", m=4),
+                    old_sb[c][:, cols].rearrange("p (n m) -> p n m", m=4),
+                    fade_ps[h], ALU.mult,
+                )
+        for c in range(2, 4):
+            nc.gpsimd.tensor_tensor(faded[c][:], old_sb[c][:], fade_sb[:], ALU.mult)
+
+        wq = sb.tile([P, PACK, I], F32, name="wq")
+        for half in range(2):
+            root = sb.tile([P, 2, I], F32, name=f"root{half}")
+            nc.scalar.activation(root[:], dens[half][:], ACT.Abs_reciprocal_sqrt)
+            share = sb.tile([P, 2, I], F32, name=f"share{half}")
+            nc.scalar.activation(share[:], root[:], ACT.Square)
+            for k in range(2):
+                nc.vector.scalar_tensor_tensor(
+                    wq[:, 2 * half + k, :].rearrange("p (n m) -> p n m", m=2),
+                    share[:, k, :].rearrange("p (n m) -> p n m", m=2),
+                    factor[half][:, k : k + 1], size_ps, ALU.mult, ALU.mult,
+                )
+        wq_grouped = sb.tile([P, I * PACK], BF16, name="wq_grouped", align_bytes=64)
+        nc.vector.tensor_copy(
+            wq_grouped[:].rearrange("p (c i r) -> p c r i", i=4, r=PACK),
+            wq[:].rearrange("p r (c i) -> p c r i", i=4),
+        )
+        wq_codes, wq_scales = quantize(wq_grouped[:], I, "wq")
+
+        tags = ["a_ps0", "a_ps1", "b_ps0", "b_ps1"]
+        for c in range(4):
+            cols = slice(c % 2 * P, (c % 2 + 1) * P)
+            grows_codes, grows_scales = grows_q[c // 2]
+            bank = ps.tile([P, 2, I], F32, name=f"gv_ps{c}", tag=tags[c])
+            nc.tensor.matmul_mx(
+                out=bank[:, 0, :],
+                lhsT=grows_codes[:, cols].bitcast(FP8X4),
+                lhsT_scale=grows_scales[:, cols],
+                rhs=wq_codes[:].bitcast(FP8X4),
+                rhs_scale=wq_scales[:],
+                start=True,
+                stop=True,
+            )
+            gv = sb.tile([P, I], F32, name=f"gv{c}")
+            nc.scalar.copy(gv[:], bank[:, 0, :])
+            nc.vector.tensor_copy(placed[c][:].indirect(offsets[:]), gv[:])
+        for c in range(4):
+            result = sb.tile([P, T], F32, name=f"result{c}")
+            engine = nc.gpsimd if c < 2 else nc.vector
+            engine.tensor_tensor(result[:], faded[c][:], placed[c][:], ALU.add)
+            nc.sync.dma_start(out[c * P : (c + 1) * P, :], result[:])

@@ -34,19 +34,6 @@ def tile_attend_bagreement_v_kernel(
         nc.sync.dma_start(offsets[:], offs)
 
         key_bytes = sb.tile([P, T], U8, name="key_bytes", align_bytes=64)
-        nc.gpsimd.memset(key_bytes[:].bitcast(I32), 0)
-        for quad in range(4):
-            nc.scalar.dma_start(
-                key_bytes[32 * quad : 32 * quad + 4, :].bitcast(I32),
-                keys_scales[0, 4 * quad : 4 * quad + 4, :].bitcast(I32),
-            )
-
-        fade_col = sb.tile([P, 2, 4], F32, name="fade_col")
-        nc.scalar.dma_start(fade_col[:], fade.rearrange("o (h p m) -> p (o h) m", h=2, m=4))
-        size_col = sb.tile([P, 2], F32, name="size_col")
-        nc.scalar.dma_start(size_col[:], size.rearrange("o (p m) -> p (o m)", m=2))
-        qs_sb = sb.tile([P, PACK], F32, name="qs_sb")
-        nc.scalar.dma_start(qs_sb[:], qs.rearrange("(p r) o -> p (r o)", r=PACK))
 
         def load_rows(src, name):
             raw = sb.tile([P, PACK, 512], F32, name=name)
@@ -54,9 +41,20 @@ def tile_attend_bagreement_v_kernel(
             return raw
 
         qa_raw = load_rows(query, "qa_raw")
+        for quad in range(4):
+            nc.sync.dma_start(
+                key_bytes[32 * quad : 32 * quad + 32, :].bitcast(I32),
+                keys_scales[0, 4 * quad : 4 * quad + 4, :].bitcast(I32).unsqueeze(0).to_broadcast([8, 4, T // 4]),
+            )
+        rows = sb.tile([P, P], F32, name="rows")
+        nc.gpsimd.memset(rows[:], 0.0)
+        nc.sync.dma_start(rows[0:8, :], fade.rearrange("o (b n) -> (o b) n", n=P))
+        nc.sync.dma_start(rows[8:10, :], size.rearrange("o (b n) -> (o b) n", n=P))
         key_words = sb.tile([P, T], I32, name="key_words", align_bytes=64)
         nc.sync.dma_start(key_words[:], keys_words[0].rearrange("p n t -> p (n t)").bitcast(I32))
         qb_raw = load_rows(query2, "qb_raw")
+        qs_sb = sb.tile([P, PACK], F32, name="qs_sb")
+        nc.sync.dma_start(qs_sb[:], qs.rearrange("(p r) o -> p (r o)", r=PACK))
         grows_raw = load_rows(grows, "grows_raw")
         old_sb = []
         for c in range(4):
@@ -73,33 +71,22 @@ def tile_attend_bagreement_v_kernel(
             nc.vector.memset(t[:], 0.0)
             placed.append(t)
 
-        fade_ps = []
-        fade_sb = sb.tile([P, T], F32, name="fade_sb")
-        for h in range(2):
-            bank = ps.tile([P, 4, P], F32, name=f"fade_ps{h}")
-            for m in range(4):
-                nc.tensor.transpose(bank[:, m, :], fade_col[:, h, m : m + 1].to_broadcast([P, P]), ident[:])
-            view = bank[:].rearrange("p m n -> p n m")
-            fade_ps.append(view)
-            nc.scalar.copy(fade_sb[:, h * BANK : (h + 1) * BANK].rearrange("p (n m) -> p n m", m=4), view)
-        size_bank = ps.tile([P, 2, P], F32, name="size_ps")
-        for m in range(2):
-            nc.tensor.transpose(size_bank[:, m, :], size_col[:, m : m + 1].to_broadcast([P, P]), ident[:])
-        size_ps = size_bank[:].rearrange("p m n -> p n m")
+        def bank_tile(n, name):
+            return ps.tile([P, BANK], F32, name=name, tag=f"bank{n}")
 
         key_scale = sb.tile([P, I], U8, name="key_scale", align_bytes=64)
         nc.vector.tensor_copy(key_scale[:], key_bytes[:].indirect(offsets[:]))
 
         def quantize(grouped, width, name):
-            codes = sb.tile([P, width], U32, name=name + "_codes", align_bytes=64)
+            codes = sb.tile([P, width], U32, name=name + "_codes", tag=name + "_codes", align_bytes=64)
             scales = sb.tile([P, width], U8, name=name + "_scales", align_bytes=64)
             nc.vector.quantize_mx(out=codes[:].bitcast(FP8X4), scales=scales[:], in_=grouped)
             return codes, scales
 
-        def deal(raw, half, name, on_vector):
-            grouped = sb.tile([P, 2 * P * PACK], BF16, name=name, align_bytes=64)
-            dst = grouped[:].rearrange("p (r s j) -> p s j r", r=2, j=PACK)
-            src = raw[:].rearrange("p j (s r) -> p s j r", r=PACK)[:, :, :, 2 * half : 2 * half + 2]
+        def deal(raw, half, name, on_vector, tag):
+            grouped = sb.tile([P, 2 * P * PACK], BF16, name=name, tag=tag, align_bytes=64)
+            dst = grouped[:].rearrange("p (r s j) -> p s r j", r=2, j=PACK)
+            src = raw[:].rearrange("p j (s r) -> p s r j", r=PACK)[:, :, 2 * half : 2 * half + 2, :]
             if on_vector:
                 nc.vector.tensor_copy(dst, src)
             else:
@@ -108,9 +95,9 @@ def tile_attend_bagreement_v_kernel(
 
         key_codes = sb.tile([P, I], U32, name="key_codes", align_bytes=64)
 
-        def scores(grouped, half, name):
+        def scores(grouped, half, name, first_bank):
             codes, scales = quantize(grouped[:], 2 * P, f"{name}{half}")
-            bank = ps.tile([P, 2, I], F32, name=f"{name}_ps{half}", tag=f"{name}_ps{half}")
+            bank = bank_tile(first_bank + half, f"{name}_ps{half}")[:].rearrange("p (k i) -> p k i", k=2)
             for k in range(2):
                 cols = slice(k * P, (k + 1) * P)
                 nc.tensor.matmul_mx(
@@ -124,108 +111,132 @@ def tile_attend_bagreement_v_kernel(
                 )
             return bank
 
-        def row_max(bank, name):
-            neg = sb.tile([P, 2], F32, name=name + "_neg")
-            pos = sb.tile([P, 2], F32, name=name + "_pos")
-            nc.vector.tensor_reduce(out=neg[:], in_=bank[:], axis=AXIS_X, op=ALU.max, negate=True)
-            nc.vector.tensor_scalar(pos[:], neg[:], -1.0, None, ALU.mult)
-            return neg, pos
+        def stats(name):
+            return sb.tile([P, PACK], F32, name=name)
 
-        def exps(bank, neg, pos, name):
-            total = sb.tile([P, 2], F32, name=name + "_sum")
-            inv = sb.tile([P, 2, I], F32, name=name + "_inv")
-            unread = sb.tile([P, 2, I], F32, name=name + "_unread")
+        def row_max(bank, neg, half):
+            nc.vector.tensor_reduce(out=neg[:, 2 * half : 2 * half + 2], in_=bank, axis=AXIS_X, op=ALU.max, negate=True)
+
+        def row_sums(banks, neg, total, half, name):
+            unread = sb.tile([P, 2, I], F32, name=f"{name}_unread{half}")
             for k in range(2):
+                r = 2 * half + k
                 nc.scalar.activation(
-                    unread[:, k, :], bank[:, k, :], ACT.Exp, bias=neg[:, k : k + 1], scale=1.0,
-                    accum_out=total[:, k : k + 1],
+                    unread[:, k, :], banks[half][:, k, :], ACT.Exp, bias=neg[:, r : r + 1], scale=1.0,
+                    accum_out=total[:, r : r + 1],
                 )
-            for k in range(2):
-                nc.scalar.activation(inv[:, k, :], bank[:, k, :], ACT.Exp, bias=pos[:, k : k + 1], scale=-1.0)
-            return total, inv
 
-        ga = [deal(qa_raw, half, f"ga{half}", half == 0) for half in range(2)]
-        nc.vector.tensor_copy(key_codes[:], key_words[:].bitcast(U32).indirect(offsets[:]))
-        a_banks = [scores(ga[half], half, "a") for half in range(2)]
-        a_max = [row_max(a_banks[half], f"amax{half}") for half in range(2)]
-        a_exp = [exps(a_banks[half], *a_max[half], f"aexp{half}") for half in range(2)]
-        b_banks = []
-        b_exp = []
-        for half in range(2):
-            bank = scores(deal(qb_raw, half, f"gb{half}", True), half, "b")
-            neg, pos = row_max(bank, f"bmax{half}")
-            b_exp.append(exps(bank, neg, pos, f"bexp{half}"))
+        def inverse_exps(banks, pos, name):
+            tiles = []
+            for r in range(PACK):
+                t = sb.tile([P, I], F32, name=f"{name}{r}", tag=f"{name}{r}", align_bytes=64)
+                nc.scalar.activation(t[:], banks[r // 2][:, r % 2, :], ACT.Exp, bias=pos[:, r : r + 1], scale=-1.0)
+                tiles.append(t)
+            return tiles
 
-        inv_sum_a = []
-        factor = []
-        for half in range(2):
-            inv = sb.tile([P, 2], F32, name=f"inv_sum_a{half}")
-            nc.vector.reciprocal(inv[:], a_exp[half][0][:])
-            fac = sb.tile([P, 2], F32, name=f"factor{half}")
-            nc.vector.tensor_tensor(fac[:], inv[:], qs_sb[:, 2 * half : 2 * half + 2], ALU.mult)
-            inv_sum_a.append(inv)
-            factor.append(fac)
-
-
-        dens = []
-        for half in range(2):
-            ratio = sb.tile([P, 2], F32, name=f"ratio{half}")
-            nc.vector.tensor_tensor(ratio[:], b_exp[half][0][:], inv_sum_a[half][:], ALU.mult)
-            den = sb.tile([P, 2, I], F32, name=f"den{half}")
-            for k in range(2):
-                nc.vector.scalar_tensor_tensor(
-                    den[:, k, :], b_exp[half][1][:, k, :], ratio[:, k : k + 1], a_exp[half][1][:, k, :],
-                    ALU.mult, ALU.add,
-                )
-            dens.append(den)
-
-        grows_q = []
-        for half in range(2):
-            grouped = sb.tile([P, 2 * P * PACK], BF16, name=f"grows_grouped{half}", align_bytes=64)
+        def group_grows(half, tag):
+            grouped = sb.tile([P, 2 * P * PACK], BF16, name=f"grows_grouped{half}", tag=tag, align_bytes=64)
             nc.vector.tensor_copy(
                 grouped[:].rearrange("p (c i j) -> p c j i", i=4, j=PACK),
                 grows_raw[:, :, half * 2 * P : (half + 1) * 2 * P].rearrange("p j (c i) -> p c j i", i=4),
             )
-            grows_q.append(quantize(grouped[:], 2 * P, f"grows{half}"))
+            return grouped
 
-        faded = [sb.tile([P, T], F32, name=f"faded{c}") for c in range(4)]
-        for c in range(2):
+        neg_a, pos_a, sum_a, inv_sum_a, factor = [stats(n) for n in ("neg_a", "pos_a", "sum_a", "inv_sum_a", "factor")]
+        neg_b, pos_b, sum_b, ratio = [stats(n) for n in ("neg_b", "pos_b", "sum_b", "ratio")]
+
+        ga = [deal(qa_raw, half, f"ga{half}", half == 0, f"ga{half}") for half in range(2)]
+        nc.vector.tensor_copy(key_codes[:], key_words[:].bitcast(U32).indirect(offsets[:]))
+        a_banks = [scores(ga[half], half, "a", 0) for half in range(2)]
+        for half in range(2):
+            row_max(a_banks[half], neg_a, half)
+            row_sums(a_banks, neg_a, sum_a, half, "a")
+        gb0 = deal(qb_raw, 0, "gb0", True, "a1_codes")
+        nc.vector.tensor_scalar(pos_a[:], neg_a[:], -1.0, None, ALU.mult)
+        gb1 = deal(qb_raw, 1, "gb1", True, "a0_codes")
+        b_banks = [scores(gb0, 0, "b", 2), scores(gb1, 1, "b", 2)]
+        row_max(b_banks[0], neg_b, 0)
+        row_sums(b_banks, neg_b, sum_b, 0, "b")
+        nc.vector.reciprocal(inv_sum_a[:], sum_a[:])
+        row_max(b_banks[1], neg_b, 1)
+        row_sums(b_banks, neg_b, sum_b, 1, "b")
+        nc.vector.tensor_tensor(factor[:], inv_sum_a[:], qs_sb[:], ALU.mult)
+        nc.vector.tensor_scalar(pos_b[:], neg_b[:], -1.0, None, ALU.mult)
+        gg0 = group_grows(0, "b1_codes")
+        inv_a = inverse_exps(a_banks, pos_a, "inv_a")
+        inv_b = inverse_exps(b_banks, pos_b, "inv_b")
+
+        turned = bank_tile(7, "turned")
+        nc.tensor.transpose(turned[:, 0:P], rows[:], ident[:])
+        cols_sb = sb.tile([P, 16], F32, name="cols_sb")
+        nc.scalar.copy(cols_sb[:], turned[:, 0:16])
+        fade_ps = []
+        for h in range(2):
+            bank = bank_tile(4 + h, f"fade_ps{h}")
+            for m in range(4):
+                b = 4 * h + m
+                nc.tensor.transpose(bank[:, m * P : (m + 1) * P], cols_sb[:, b : b + 1].to_broadcast([P, P]), ident[:])
+            fade_ps.append(bank)
+        size_ps = bank_tile(6, "size_ps")
+        for m in range(2):
+            nc.tensor.transpose(size_ps[:, m * P : (m + 1) * P], cols_sb[:, 8 + m : 9 + m].to_broadcast([P, P]), ident[:])
+
+
+        grows_q = [quantize(gg0[:], 2 * P, "grows0")]
+        nc.vector.tensor_tensor(ratio[:], sum_b[:], inv_sum_a[:], ALU.mult)
+        dens = []
+        for r in range(PACK):
+            den = sb.tile([P, I], F32, name=f"den{r}")
+            nc.vector.scalar_tensor_tensor(den[:], inv_b[r][:], ratio[:, r : r + 1], inv_a[r][:], ALU.mult, ALU.add)
+            dens.append(den)
+        gg1 = group_grows(1, "inv_a0")
+        grows_q.append(quantize(gg1[:], 2 * P, "grows1"))
+
+        def fade_on_vector(c, tag):
+            t = sb.tile([P, T], F32, name=f"faded{c}", tag=tag, align_bytes=64)
             for h in range(2):
                 cols = slice(h * BANK, (h + 1) * BANK)
-                nc.vector.tensor_tensor(
-                    faded[c][:, cols].rearrange("p (n m) -> p n m", m=4),
-                    old_sb[c][:, cols].rearrange("p (n m) -> p n m", m=4),
-                    fade_ps[h], ALU.mult,
-                )
-        for c in range(2, 4):
-            nc.gpsimd.tensor_tensor(faded[c][:], old_sb[c][:], fade_sb[:], ALU.mult)
+                nc.vector.tensor_tensor(t[:, cols], old_sb[c][:, cols], fade_ps[h][:], ALU.mult)
+            return t
 
-        wq = sb.tile([P, PACK, I], F32, name="wq")
-        for half in range(2):
-            root = sb.tile([P, 2, I], F32, name=f"root{half}")
-            nc.scalar.activation(root[:], dens[half][:], ACT.Abs_reciprocal_sqrt)
-            share = sb.tile([P, 2, I], F32, name=f"share{half}")
-            nc.scalar.activation(share[:], root[:], ACT.Square)
-            for k in range(2):
+        wq = sb.tile([P, PACK, I], F32, name="wq", tag="wq", align_bytes=64)
+        roots = []
+        for step in range(PACK + 1):
+            if step < PACK:
+                root = sb.tile([P, I], F32, name=f"root{step}")
+                nc.scalar.activation(root[:], dens[step][:], ACT.Abs_reciprocal_sqrt)
+                roots.append(root)
+            if step > 0:
+                r = step - 1
+                share = sb.tile([P, I], F32, name=f"share{r}")
+                nc.scalar.activation(share[:], roots[r][:], ACT.Square)
                 nc.vector.scalar_tensor_tensor(
-                    wq[:, 2 * half + k, :].rearrange("p (n m) -> p n m", m=2),
-                    share[:, k, :].rearrange("p (n m) -> p n m", m=2),
-                    factor[half][:, k : k + 1], size_ps, ALU.mult, ALU.mult,
+                    wq[:, r, :], share[:], factor[:, r : r + 1], size_ps[:, 0:I], ALU.mult, ALU.mult
                 )
-        wq_grouped = sb.tile([P, I * PACK], BF16, name="wq_grouped", align_bytes=64)
-        nc.vector.tensor_copy(
-            wq_grouped[:].rearrange("p (c i r) -> p c r i", i=4, r=PACK),
-            wq[:].rearrange("p r (c i) -> p c r i", i=4),
-        )
-        wq_codes, wq_scales = quantize(wq_grouped[:], I, "wq")
+        wq_grouped = sb.tile([P, I * PACK], BF16, name="wq_grouped", tag="wq_grouped", align_bytes=64)
+        wq_codes = sb.tile([P, I], U32, name="wq_codes", align_bytes=64)
+        wq_scales = sb.tile([P, I], U8, name="wq_scales", align_bytes=64)
+        for h in range(2):
+            nc.vector.tensor_copy(
+                wq_grouped[:, h * BANK : (h + 1) * BANK].rearrange("p (c i r) -> p c r i", i=4, r=PACK),
+                wq[:, :, h * P : (h + 1) * P].rearrange("p r (c i) -> p c r i", i=4),
+            )
+        for h in range(2):
+            cols = slice(h * P, (h + 1) * P)
+            nc.vector.quantize_mx(
+                out=wq_codes[:, cols].bitcast(FP8X4), scales=wq_scales[:, cols],
+                in_=wq_grouped[:, h * BANK : (h + 1) * BANK],
+            )
 
-        tags = ["a_ps0", "a_ps1", "b_ps0", "b_ps1"]
+        faded = [fade_on_vector(0, "inv_a3"), fade_on_vector(1, "wq")]
+
+        gv = []
         for c in range(4):
             cols = slice(c % 2 * P, (c % 2 + 1) * P)
             grows_codes, grows_scales = grows_q[c // 2]
-            bank = ps.tile([P, 2, I], F32, name=f"gv_ps{c}", tag=tags[c])
+            bank = bank_tile(c % 2, f"gv_ps{c}")
             nc.tensor.matmul_mx(
-                out=bank[:, 0, :],
+                out=bank[:, 0:I],
                 lhsT=grows_codes[:, cols].bitcast(FP8X4),
                 lhsT_scale=grows_scales[:, cols],
                 rhs=wq_codes[:].bitcast(FP8X4),
@@ -233,11 +244,44 @@ def tile_attend_bagreement_v_kernel(
                 start=True,
                 stop=True,
             )
-            gv = sb.tile([P, I], F32, name=f"gv{c}")
-            nc.scalar.copy(gv[:], bank[:, 0, :])
-            nc.vector.tensor_copy(placed[c][:].indirect(offsets[:]), gv[:])
-        for c in range(4):
+            t = sb.tile([P, I], F32, name=f"gv{c}")
+            nc.scalar.copy(t[:], bank[:, 0:I])
+            gv.append(t)
+
+        result_bank = {(2, 0): 7, (2, 1): 6, (3, 0): 4, (3, 1): 5}
+        faded_ps = {}
+        for h in range(2):
+            turned_sb = sb.tile([P, 4, 2, P], F32, name=f"turned{h}", tag=("wq_grouped", "turned1")[h], align_bytes=64)
+            for pair in range(2):
+                stage = bank_tile(2 + pair, f"stage{h}{pair}")[:].rearrange("p (b c e) -> p b c e", b=2, c=2)
+                for b in range(2):
+                    blk = 4 * h + 2 * pair + b
+                    for c in range(2):
+                        nc.tensor.transpose(stage[:, b, c, :], old_sb[2 + c][:, blk * P : (blk + 1) * P], ident[:])
+                for b in range(2):
+                    blk = 4 * h + 2 * pair + b
+                    nc.scalar.activation(
+                        turned_sb[:, 2 * pair + b, :, :], stage[:, b, :, :], ACT.Copy, scale=cols_sb[:, blk : blk + 1]
+                    )
+            for c in range(2):
+                bank = bank_tile(result_bank[(2 + c, h)], f"faded_ps{c}{h}")
+                for m in range(4):
+                    nc.tensor.transpose(bank[:, m * P : (m + 1) * P], turned_sb[:, m, c, :], ident[:])
+                faded_ps[(2 + c, h)] = bank
+
+        def finish(c):
             result = sb.tile([P, T], F32, name=f"result{c}")
-            engine = nc.gpsimd if c < 2 else nc.vector
-            engine.tensor_tensor(result[:], faded[c][:], placed[c][:], ALU.add)
-            nc.sync.dma_start(out[c * P : (c + 1) * P, :], result[:])
+            rows_out = out[c * P : (c + 1) * P, :]
+            if c < 2:
+                nc.gpsimd.tensor_tensor(result[:], faded[c][:], placed[c][:], ALU.add)
+                nc.sync.dma_start(rows_out, result[:])
+            else:
+                for h in range(2):
+                    cols = slice(h * BANK, (h + 1) * BANK)
+                    nc.vector.tensor_tensor(result[:, cols], faded_ps[(c, h)][:], placed[c][:, cols], ALU.add)
+                    nc.sync.dma_start(rows_out[:, cols], result[:, cols])
+
+        for c in range(4):
+            nc.vector.tensor_copy(placed[c][:].indirect(offsets[:]), gv[c][:])
+        for c in range(4):
+            finish(c)

@@ -20,6 +20,18 @@ AXIS_X = mybir.AxisListType.X
 P = 128
 PACK = 4
 BANK = 512
+QUADRANT = 32
+E_TILES = E // P
+T_BLOCKS = T // P
+I_BLOCKS = I // P
+ON_GPSIMD = 2
+TINY = 1e-30
+
+BANKS_A = (0, 1)
+BANKS_B = (2, 3)
+BANKS_FADE = (4, 5)
+BANK_SIZE = 6
+BANK_TURN = 7
 
 
 def tile_attend_bagreement_v_kernel(
@@ -30,258 +42,266 @@ def tile_attend_bagreement_v_kernel(
         sb = ctx.enter_context(tc.tile_pool(name="sb", bufs=1))
         ps = ctx.enter_context(tc.psum_pool(name="ps", bufs=1))
 
-        offsets = sb.tile([P, I // 16], U16, name="offsets")
-        nc.sync.dma_start(offsets[:], offs)
+        def sbuf(shape, dtype, name, tag=None):
+            return sb.tile(shape, dtype, name=name, tag=tag or name, align_bytes=64)
 
-        key_bytes = sb.tile([P, T], U8, name="key_bytes", align_bytes=64)
+        def psum(bank, name):
+            return ps.tile([P, BANK], F32, name=name, tag=f"bank{bank}")
 
-        def load_rows(src, name):
-            raw = sb.tile([P, PACK, 512], F32, name=name)
+        def half_of(h, width):
+            return slice(h * width // 2, (h + 1) * width // 2)
+
+        def block(n):
+            return slice(n * P, (n + 1) * P)
+
+        def load_k_first(src, name):
+            raw = sbuf([P, PACK, src.shape[1]], F32, name)
             nc.sync.dma_start(raw[:], src.rearrange("(p j) c -> p j c", j=PACK))
             return raw
 
-        qa_raw = load_rows(query, "qa_raw")
-        for quad in range(4):
-            nc.sync.dma_start(
-                key_bytes[32 * quad : 32 * quad + 32, :].bitcast(I32),
-                keys_scales[0, 4 * quad : 4 * quad + 4, :].bitcast(I32).unsqueeze(0).to_broadcast([8, 4, T // 4]),
-            )
-        rows = sb.tile([P, P], F32, name="rows")
-        nc.gpsimd.memset(rows[:], 0.0)
-        nc.sync.dma_start(rows[0:8, :], fade.rearrange("o (b n) -> (o b) n", n=P))
-        nc.sync.dma_start(rows[8:10, :], size.rearrange("o (b n) -> (o b) n", n=P))
-        key_words = sb.tile([P, T], I32, name="key_words", align_bytes=64)
-        nc.sync.dma_start(key_words[:], keys_words[0].rearrange("p n t -> p (n t)").bitcast(I32))
-        qb_raw = load_rows(query2, "qb_raw")
-        qs_sb = sb.tile([P, PACK], F32, name="qs_sb")
-        nc.sync.dma_start(qs_sb[:], qs.rearrange("(p r) o -> p (r o)", r=PACK))
-        grows_raw = load_rows(grows, "grows_raw")
-        old_sb = []
-        for c in range(4):
-            t = sb.tile([P, T], F32, name=f"old{c}")
-            nc.sync.dma_start(t[:], old[c * P : (c + 1) * P, :])
-            old_sb.append(t)
+        def load_old(c):
+            rows_of_old = sbuf([P, T], F32, f"old{c}")
+            nc.sync.dma_start(rows_of_old[:], old[block(c), :])
+            return rows_of_old
 
-        ident = sb.tile([P, P], F32, name="ident")
+        offsets = sb.tile([P, I // 16], U16, name="offsets")
+        nc.sync.dma_start(offsets[:], offs)
+        qa_raw = load_k_first(query, "qa_raw")
+
+        key_bytes = sbuf([P, T], U8, "key_bytes")
+        for u in range(P // QUADRANT):
+            four_rows = keys_scales[0, 4 * u : 4 * u + 4, :].bitcast(I32)
+            nc.sync.dma_start(
+                key_bytes[QUADRANT * u : QUADRANT * (u + 1), :].bitcast(I32),
+                four_rows.unsqueeze(0).to_broadcast([QUADRANT // 4, 4, T // 4]),
+            )
+
+        rows = sbuf([P, P], F32, "rows")
+        nc.gpsimd.memset(rows[:], 0.0)
+        nc.sync.dma_start(rows[0:T_BLOCKS, :], fade.rearrange("o (b n) -> (o b) n", n=P))
+        nc.sync.dma_start(rows[T_BLOCKS : T_BLOCKS + I_BLOCKS, :], size.rearrange("o (b n) -> (o b) n", n=P))
+
+        key_words = sbuf([P, T], I32, "key_words")
+        nc.sync.dma_start(key_words[:], keys_words[0].rearrange("p n t -> p (n t)").bitcast(I32))
+        qb_raw = [load_k_first(query2[:, half_of(h, Q)], f"qb_raw{h}") for h in range(2)]
+        qs_sb = sbuf([P, PACK], F32, "qs_sb")
+        nc.sync.dma_start(qs_sb[:], qs.rearrange("(p r) o -> p (r o)", r=PACK))
+        grows_raw = [load_k_first(grows[:, half_of(0, E)], "grows_raw0")]
+        old_sb = [load_old(0)]
+        grows_raw.append(load_k_first(grows[:, half_of(1, E)], "grows_raw1"))
+        old_sb.extend(load_old(c) for c in range(1, E_TILES))
+
+        ident = sbuf([P, P], F32, "ident")
         make_identity(nc, ident[:])
 
-        placed = []
-        for c in range(4):
-            t = sb.tile([P, T], F32, name=f"placed{c}")
-            nc.vector.memset(t[:], 0.0)
-            placed.append(t)
+        placed = [sbuf([P, T], F32, f"placed{c}") for c in range(E_TILES)]
+        for window in placed:
+            nc.vector.memset(window[:], 0.0)
 
-        def bank_tile(n, name):
-            return ps.tile([P, BANK], F32, name=name, tag=f"bank{n}")
-
-        key_scale = sb.tile([P, I], U8, name="key_scale", align_bytes=64)
-        nc.vector.tensor_copy(key_scale[:], key_bytes[:].indirect(offsets[:]))
-
-        def quantize(grouped, width, name):
-            codes = sb.tile([P, width], U32, name=name + "_codes", tag=name + "_codes", align_bytes=64)
-            scales = sb.tile([P, width], U8, name=name + "_scales", align_bytes=64)
+        def quantize(grouped, name, tag=None):
+            words = grouped.shape[1] // PACK
+            codes = sbuf([P, words], U32, name + "_codes", tag)
+            scales = sbuf([P, words], U8, name + "_scales")
             nc.vector.quantize_mx(out=codes[:].bitcast(FP8X4), scales=scales[:], in_=grouped)
             return codes, scales
 
-        def deal(raw, half, name, on_vector, tag):
-            grouped = sb.tile([P, 2 * P * PACK], BF16, name=name, tag=tag, align_bytes=64)
-            dst = grouped[:].rearrange("p (r s j) -> p s r j", r=2, j=PACK)
-            src = raw[:].rearrange("p j (s r) -> p s r j", r=PACK)[:, :, 2 * half : 2 * half + 2, :]
-            if on_vector:
-                nc.vector.tensor_copy(dst, src)
-            else:
-                nc.scalar.copy(dst, src)
-            return grouped
-
-        key_codes = sb.tile([P, I], U32, name="key_codes", align_bytes=64)
-
-        def scores(grouped, half, name, first_bank):
-            codes, scales = quantize(grouped[:], 2 * P, f"{name}{half}")
-            bank = bank_tile(first_bank + half, f"{name}_ps{half}")[:].rearrange("p (k i) -> p k i", k=2)
-            for k in range(2):
-                cols = slice(k * P, (k + 1) * P)
-                nc.tensor.matmul_mx(
-                    out=bank[:, k, :],
-                    lhsT=codes[:, cols].bitcast(FP8X4),
-                    lhsT_scale=scales[:, cols],
-                    rhs=key_codes[:].bitcast(FP8X4),
-                    rhs_scale=key_scale[:],
-                    start=True,
-                    stop=True,
-                )
-            return bank
-
-        def stats(name):
-            return sb.tile([P, PACK], F32, name=name)
-
-        def row_max(bank, neg, half):
-            nc.vector.tensor_reduce(out=neg[:, 2 * half : 2 * half + 2], in_=bank, axis=AXIS_X, op=ALU.max, negate=True)
-
-        def row_sums(banks, neg, total, half, name):
-            unread = sb.tile([P, 2, I], F32, name=f"{name}_unread{half}")
-            for k in range(2):
-                r = 2 * half + k
-                nc.scalar.activation(
-                    unread[:, k, :], banks[half][:, k, :], ACT.Exp, bias=neg[:, r : r + 1], scale=1.0,
-                    accum_out=total[:, r : r + 1],
-                )
-
-        def inverse_exps(banks, pos, name):
-            tiles = []
-            for r in range(PACK):
-                t = sb.tile([P, I], F32, name=f"{name}{r}", tag=f"{name}{r}", align_bytes=64)
-                nc.scalar.activation(t[:], banks[r // 2][:, r % 2, :], ACT.Exp, bias=pos[:, r : r + 1], scale=-1.0)
-                tiles.append(t)
-            return tiles
-
-        def group_grows(half, tag):
-            grouped = sb.tile([P, 2 * P * PACK], BF16, name=f"grows_grouped{half}", tag=tag, align_bytes=64)
-            nc.vector.tensor_copy(
-                grouped[:].rearrange("p (c i j) -> p c j i", i=4, j=PACK),
-                grows_raw[:, :, half * 2 * P : (half + 1) * 2 * P].rearrange("p j (c i) -> p c j i", i=4),
-            )
-            return grouped
-
-        neg_a, pos_a, sum_a, inv_sum_a, factor = [stats(n) for n in ("neg_a", "pos_a", "sum_a", "inv_sum_a", "factor")]
-        neg_b, pos_b, sum_b, ratio = [stats(n) for n in ("neg_b", "pos_b", "sum_b", "ratio")]
-
-        ga = [deal(qa_raw, half, f"ga{half}", half == 0, f"ga{half}") for half in range(2)]
-        nc.vector.tensor_copy(key_codes[:], key_words[:].bitcast(U32).indirect(offsets[:]))
-        a_banks = [scores(ga[half], half, "a", 0) for half in range(2)]
-        for half in range(2):
-            row_max(a_banks[half], neg_a, half)
-            row_sums(a_banks, neg_a, sum_a, half, "a")
-        gb0 = deal(qb_raw, 0, "gb0", True, "a1_codes")
-        nc.vector.tensor_scalar(pos_a[:], neg_a[:], -1.0, None, ALU.mult)
-        gb1 = deal(qb_raw, 1, "gb1", True, "a0_codes")
-        b_banks = [scores(gb0, 0, "b", 2), scores(gb1, 1, "b", 2)]
-        row_max(b_banks[0], neg_b, 0)
-        row_sums(b_banks, neg_b, sum_b, 0, "b")
-        nc.vector.reciprocal(inv_sum_a[:], sum_a[:])
-        row_max(b_banks[1], neg_b, 1)
-        row_sums(b_banks, neg_b, sum_b, 1, "b")
-        nc.vector.tensor_tensor(factor[:], inv_sum_a[:], qs_sb[:], ALU.mult)
-        nc.vector.tensor_scalar(pos_b[:], neg_b[:], -1.0, None, ALU.mult)
-        gg0 = group_grows(0, "b1_codes")
-        inv_a = inverse_exps(a_banks, pos_a, "inv_a")
-        inv_b = inverse_exps(b_banks, pos_b, "inv_b")
-
-        turned = bank_tile(7, "turned")
-        nc.tensor.transpose(turned[:, 0:P], rows[:], ident[:])
-        cols_sb = sb.tile([P, 16], F32, name="cols_sb")
-        nc.scalar.copy(cols_sb[:], turned[:, 0:16])
-        fade_ps = []
-        for h in range(2):
-            bank = bank_tile(4 + h, f"fade_ps{h}")
-            for m in range(4):
-                b = 4 * h + m
-                nc.tensor.transpose(bank[:, m * P : (m + 1) * P], cols_sb[:, b : b + 1].to_broadcast([P, P]), ident[:])
-            fade_ps.append(bank)
-        size_ps = bank_tile(6, "size_ps")
-        for m in range(2):
-            nc.tensor.transpose(size_ps[:, m * P : (m + 1) * P], cols_sb[:, 8 + m : 9 + m].to_broadcast([P, P]), ident[:])
-
-
-        grows_q = [quantize(gg0[:], 2 * P, "grows0")]
-        nc.vector.tensor_tensor(ratio[:], sum_b[:], inv_sum_a[:], ALU.mult)
-        dens = []
-        for r in range(PACK):
-            den = sb.tile([P, I], F32, name=f"den{r}")
-            nc.vector.scalar_tensor_tensor(den[:], inv_b[r][:], ratio[:, r : r + 1], inv_a[r][:], ALU.mult, ALU.add)
-            dens.append(den)
-        gg1 = group_grows(1, "inv_a0")
-        grows_q.append(quantize(gg1[:], 2 * P, "grows1"))
-
-        def fade_on_vector(c, tag):
-            t = sb.tile([P, T], F32, name=f"faded{c}", tag=tag, align_bytes=64)
-            for h in range(2):
-                cols = slice(h * BANK, (h + 1) * BANK)
-                nc.vector.tensor_tensor(t[:, cols], old_sb[c][:, cols], fade_ps[h][:], ALU.mult)
-            return t
-
-        wq = sb.tile([P, PACK, I], F32, name="wq", tag="wq", align_bytes=64)
-        roots = []
-        for step in range(PACK + 1):
-            if step < PACK:
-                root = sb.tile([P, I], F32, name=f"root{step}")
-                nc.scalar.activation(root[:], dens[step][:], ACT.Abs_reciprocal_sqrt)
-                roots.append(root)
-            if step > 0:
-                r = step - 1
-                share = sb.tile([P, I], F32, name=f"share{r}")
-                nc.scalar.activation(share[:], roots[r][:], ACT.Square)
-                nc.vector.scalar_tensor_tensor(
-                    wq[:, r, :], share[:], factor[:, r : r + 1], size_ps[:, 0:I], ALU.mult, ALU.mult
-                )
-        wq_grouped = sb.tile([P, I * PACK], BF16, name="wq_grouped", tag="wq_grouped", align_bytes=64)
-        wq_codes = sb.tile([P, I], U32, name="wq_codes", align_bytes=64)
-        wq_scales = sb.tile([P, I], U8, name="wq_scales", align_bytes=64)
-        for h in range(2):
-            nc.vector.tensor_copy(
-                wq_grouped[:, h * BANK : (h + 1) * BANK].rearrange("p (c i r) -> p c r i", i=4, r=PACK),
-                wq[:, :, h * P : (h + 1) * P].rearrange("p r (c i) -> p c r i", i=4),
-            )
-        for h in range(2):
-            cols = slice(h * P, (h + 1) * P)
-            nc.vector.quantize_mx(
-                out=wq_codes[:, cols].bitcast(FP8X4), scales=wq_scales[:, cols],
-                in_=wq_grouped[:, h * BANK : (h + 1) * BANK],
-            )
-
-        faded = [fade_on_vector(0, "inv_a3"), fade_on_vector(1, "wq")]
-
-        gv = []
-        for c in range(4):
-            cols = slice(c % 2 * P, (c % 2 + 1) * P)
-            grows_codes, grows_scales = grows_q[c // 2]
-            bank = bank_tile(c % 2, f"gv_ps{c}")
+        def product(dst, lhs_codes, lhs_scales, rhs_codes, rhs_scales):
             nc.tensor.matmul_mx(
-                out=bank[:, 0:I],
-                lhsT=grows_codes[:, cols].bitcast(FP8X4),
-                lhsT_scale=grows_scales[:, cols],
-                rhs=wq_codes[:].bitcast(FP8X4),
-                rhs_scale=wq_scales[:],
+                out=dst,
+                lhsT=lhs_codes.bitcast(FP8X4),
+                lhsT_scale=lhs_scales,
+                rhs=rhs_codes.bitcast(FP8X4),
+                rhs_scale=rhs_scales,
                 start=True,
                 stop=True,
             )
-            t = sb.tile([P, I], F32, name=f"gv{c}")
-            nc.scalar.copy(t[:], bank[:, 0:I])
-            gv.append(t)
 
-        result_bank = {(2, 0): 7, (2, 1): 6, (3, 0): 4, (3, 1): 5}
-        faded_ps = {}
+        def scores(grouped, bank, name):
+            codes, scales = quantize(grouped, name)
+            pair = psum(bank, name + "_ps")[:].rearrange("p (k i) -> p k i", k=2)
+            for k in range(2):
+                product(pair[:, k, :], codes[:, block(k)], scales[:, block(k)], key_codes[:], key_scales[:])
+            return pair
+
+        def softmax_terms(pair, neg_max, total, h, name, tag=None):
+            nc.vector.tensor_reduce(out=neg_max[:, half_of(h, PACK)], in_=pair, axis=AXIS_X, op=ALU.max, negate=True)
+            terms = sbuf([P, 2, I], F32, name, tag)
+            for k in range(2):
+                r = 2 * h + k
+                nc.scalar.activation(
+                    terms[:, k, :], pair[:, k, :], ACT.Exp, bias=neg_max[:, r : r + 1], scale=1.0,
+                    accum_out=total[:, r : r + 1],
+                )
+            return terms
+
+        def interleave(engine_copy, grouped, raw):
+            engine_copy(
+                grouped.rearrange("p (c i j) -> p c j i", i=4, j=PACK),
+                raw.rearrange("p j (c i) -> p c j i", i=4),
+            )
+
+        key_scales = sbuf([P, I], U8, "key_scales")
+        nc.vector.tensor_copy(key_scales[:], key_bytes[:].indirect(offsets[:]))
+
+        qa_dealt = qa_raw[:].rearrange("p j (s r) -> p s r j", r=PACK)
+        qa_grouped = []
+        for h, engine_copy in enumerate((nc.vector.tensor_copy, nc.scalar.copy)):
+            grouped = sbuf([P, 2 * P * PACK], BF16, f"qa_grouped{h}")
+            engine_copy(
+                grouped[:].rearrange("p (r s j) -> p s r j", r=2, j=PACK), qa_dealt[:, :, half_of(h, PACK), :]
+            )
+            qa_grouped.append(grouped)
+
+        key_codes = sbuf([P, I], U32, "key_codes")
+        nc.vector.tensor_copy(key_codes[:], key_words[:].bitcast(U32).indirect(offsets[:]))
+
+        turned_rows = psum(BANK_TURN, "turned_rows")
+        nc.tensor.transpose(turned_rows[:, 0:P], rows[:], ident[:])
+        columns = sbuf([P, T_BLOCKS + I_BLOCKS], F32, "columns")
+        nc.scalar.copy(columns[:], turned_rows[:, 0 : T_BLOCKS + I_BLOCKS])
+
+        def spread(dst, b):
+            nc.tensor.transpose(dst, columns[:, b : b + 1].to_broadcast([P, P]), ident[:])
+
+        fade_sb = sbuf([P, T], F32, "fade_sb")
         for h in range(2):
-            turned_sb = sb.tile([P, 4, 2, P], F32, name=f"turned{h}", tag=("wq_grouped", "turned1")[h], align_bytes=64)
-            for pair in range(2):
-                stage = bank_tile(2 + pair, f"stage{h}{pair}")[:].rearrange("p (b c e) -> p b c e", b=2, c=2)
+            fade_ps = psum(BANKS_FADE[h], f"fade_ps{h}")
+            for m in range(T_BLOCKS // 2):
+                spread(fade_ps[:, block(m)], h * T_BLOCKS // 2 + m)
+            nc.scalar.copy(fade_sb[:, half_of(h, T)], fade_ps[:])
+        size_ps = psum(BANK_SIZE, "size_ps")
+        for m in range(I_BLOCKS):
+            spread(size_ps[:, block(m)], T_BLOCKS + m)
+
+        neg_max_a, sum_a, inv_sum_a, neg_max_b, sum_b = [
+            sbuf([P, PACK], F32, name) for name in ("neg_max_a", "sum_a", "inv_sum_a", "neg_max_b", "sum_b")
+        ]
+        a_pairs = [scores(qa_grouped[h][:], BANKS_A[h], f"a{h}") for h in range(2)]
+
+        qb_grouped = sbuf([P, Q * PACK], BF16, "qb_grouped")
+        qb_view = qb_grouped[:].rearrange("p (r s j) -> p s r j", r=PACK, j=PACK)
+        qb_dealt = [raw[:].rearrange("p j (s r) -> p s r j", r=PACK) for raw in qb_raw]
+        nc.scalar.copy(qb_view[:, half_of(0, P)], qb_dealt[0])
+        pa = [softmax_terms(a_pairs[h], neg_max_a, sum_a, h, f"pa{h}") for h in range(2)]
+        nc.vector.tensor_copy(qb_view[:, half_of(1, P)], qb_dealt[1])
+        b_pairs = [scores(qb_grouped[:, half_of(h, Q * PACK)], BANKS_B[h], f"b{h}") for h in range(2)]
+        nc.vector.reciprocal(inv_sum_a[:], sum_a[:])
+
+        grows_grouped = [sbuf([P, E // 2 * PACK], BF16, "grows_grouped0")]
+        interleave(nc.scalar.copy, grows_grouped[0][:], grows_raw[0][:])
+        pb = [
+            softmax_terms(b_pairs[h], neg_max_b, sum_b, h, f"pb{h}", tag)
+            for h, tag in enumerate(("grows_raw0", None))
+        ]
+
+        def fade_on_gpsimd(c, tag):
+            result = sbuf([P, T], F32, f"faded{c}", tag)
+            for h in range(2):
+                cols = half_of(h, T)
+                nc.gpsimd.tensor_tensor(result[:, cols], old_sb[c][:, cols], fade_sb[:, cols], ALU.mult)
+            return result
+
+        faded = [fade_on_gpsimd(0, "qb_grouped")]
+
+        weighted = [sbuf([P, 2, I], F32, f"weighted{h}", f"b{h}_codes") for h in range(2)]
+        for r in range(PACK):
+            nc.vector.scalar_tensor_tensor(
+                weighted[r // 2][:, r % 2, :], pa[r // 2][:, r % 2, :], qs_sb[:, r : r + 1], size_ps[:, 0:I],
+                ALU.mult, ALU.mult,
+            )
+        dens = []
+        for h in range(2):
+            ratio = sbuf([P, 2], F32, f"ratio{h}")
+            nc.vector.tensor_tensor(ratio[:], sum_b[:, half_of(h, PACK)], inv_sum_a[:, half_of(h, PACK)], ALU.mult)
+            for k in range(2):
+                den = sbuf([P, I], F32, f"den{2 * h + k}")
+                nc.vector.scalar_tensor_tensor(
+                    den[:], pa[h][:, k, :], ratio[:, k : k + 1], pb[h][:, k, :], ALU.mult, ALU.add
+                )
+                dens.append(den)
+        nums = []
+        for h in range(2):
+            num = sbuf([P, 2, I], F32, f"num{h}")
+            nc.vector.tensor_tensor(num[:], weighted[h][:], pb[h][:], ALU.mult)
+            nums.append(num)
+
+        def grows_columns(c):
+            return grows_grouped[c // 2][:, half_of(c % 2, E // 2 * PACK)]
+
+        grows_q = [quantize(grows_columns(0), "grows0")]
+
+        wq = sbuf([P, PACK, I], F32, "wq")
+        roots = []
+        for step in range(PACK + 1):
+            if step < PACK:
+                root = sbuf([P, I], F32, f"root{step}")
+                nc.scalar.activation(
+                    root[:], dens[step][:], ACT.Abs_reciprocal_sqrt, bias=TINY, scale=sum_a[:, step : step + 1]
+                )
+                roots.append(root)
+            if step > 0:
+                r = step - 1
+                inverse = sbuf([P, I], F32, f"inverse{r}")
+                nc.scalar.activation(inverse[:], roots[r][:], ACT.Square)
+                nc.vector.tensor_tensor(wq[:, r, :], inverse[:], nums[r // 2][:, r % 2, :], ALU.mult)
+
+        last_root = f"root{PACK - 1}"
+        grows_grouped.append(sbuf([P, E // 2 * PACK], BF16, "grows_grouped1", last_root))
+        interleave(nc.scalar.copy, grows_grouped[1][:], grows_raw[1][:])
+
+        wq_grouped = sbuf([P, I * PACK], BF16, "wq_grouped")
+        wq_codes = sbuf([P, I], U32, "wq_codes")
+        wq_scales = sbuf([P, I], U8, "wq_scales")
+        for m in range(I_BLOCKS):
+            interleave(nc.vector.tensor_copy, wq_grouped[:, half_of(m, I * PACK)], wq[:, :, block(m)])
+        for m in range(I_BLOCKS):
+            nc.vector.quantize_mx(
+                out=wq_codes[:, block(m)].bitcast(FP8X4),
+                scales=wq_scales[:, block(m)],
+                in_=wq_grouped[:, half_of(m, I * PACK)],
+            )
+
+        for c in range(1, E_TILES):
+            grows_q.append(quantize(grows_columns(c), f"grows{c}", "wq" if c == 1 else None))
+        faded.append(fade_on_gpsimd(1, last_root))
+
+        gv = []
+        for c in range(E_TILES):
+            gv_ps = psum(BANKS_A[c % 2], f"gv_ps{c}")
+            product(gv_ps[:, 0:I], grows_q[c][0][:], grows_q[c][1][:], wq_codes[:], wq_scales[:])
+            gv_sb = sbuf([P, I], F32, f"gv{c}")
+            nc.scalar.copy(gv_sb[:], gv_ps[:, 0:I])
+            gv.append(gv_sb)
+
+        faded_banks = {2: (BANK_TURN, BANK_SIZE), 3: BANKS_FADE}
+        faded_ps = {}
+        for h, tag in enumerate(("wq_codes", None)):
+            turned = sbuf([P, T_BLOCKS // 2, 2, P], F32, f"turned{h}", tag)
+            for n in range(2):
+                stage = psum(BANKS_B[n], f"stage{h}{n}")[:].rearrange("p (b c e) -> p b c e", b=2, c=2)
+                first = h * T_BLOCKS // 2 + 2 * n
                 for b in range(2):
-                    blk = 4 * h + 2 * pair + b
                     for c in range(2):
-                        nc.tensor.transpose(stage[:, b, c, :], old_sb[2 + c][:, blk * P : (blk + 1) * P], ident[:])
+                        nc.tensor.transpose(stage[:, b, c, :], old_sb[ON_GPSIMD + c][:, block(first + b)], ident[:])
                 for b in range(2):
-                    blk = 4 * h + 2 * pair + b
                     nc.scalar.activation(
-                        turned_sb[:, 2 * pair + b, :, :], stage[:, b, :, :], ACT.Copy, scale=cols_sb[:, blk : blk + 1]
+                        turned[:, 2 * n + b, :, :], stage[:, b, :, :], ACT.Copy,
+                        scale=columns[:, first + b : first + b + 1],
                     )
-            for c in range(2):
-                bank = bank_tile(result_bank[(2 + c, h)], f"faded_ps{c}{h}")
-                for m in range(4):
-                    nc.tensor.transpose(bank[:, m * P : (m + 1) * P], turned_sb[:, m, c, :], ident[:])
-                faded_ps[(2 + c, h)] = bank
+            for c in range(ON_GPSIMD, E_TILES):
+                back = psum(faded_banks[c][h], f"faded_ps{c}{h}")
+                for m in range(T_BLOCKS // 2):
+                    nc.tensor.transpose(back[:, block(m)], turned[:, m, c - ON_GPSIMD, :], ident[:])
+                faded_ps[(c, h)] = back
 
-        def finish(c):
-            result = sb.tile([P, T], F32, name=f"result{c}")
-            rows_out = out[c * P : (c + 1) * P, :]
-            if c < 2:
-                nc.gpsimd.tensor_tensor(result[:], faded[c][:], placed[c][:], ALU.add)
-                nc.sync.dma_start(rows_out, result[:])
-            else:
-                for h in range(2):
-                    cols = slice(h * BANK, (h + 1) * BANK)
-                    nc.vector.tensor_tensor(result[:, cols], faded_ps[(c, h)][:], placed[c][:, cols], ALU.add)
-                    nc.sync.dma_start(rows_out[:, cols], result[:, cols])
-
-        for c in range(4):
+        for c in range(E_TILES):
             nc.vector.tensor_copy(placed[c][:].indirect(offsets[:]), gv[c][:])
-        for c in range(4):
-            finish(c)
+        for c in range(E_TILES):
+            result = sbuf([P, T], F32, f"result{c}")
+            for h in range(2):
+                cols = half_of(h, T)
+                if c < ON_GPSIMD:
+                    nc.gpsimd.tensor_tensor(result[:, cols], faded[c][:, cols], placed[c][:, cols], ALU.add)
+                else:
+                    nc.vector.tensor_tensor(result[:, cols], faded_ps[(c, h)][:], placed[c][:, cols], ALU.add)
+                nc.sync.dma_start(out[block(c), cols], result[:, cols])

from contextlib import ExitStack

import concourse.mybir as mybir
from concourse.masks import make_identity

D, E, T, I, Q = 512, 512, 1024, 256, 512
FLOPS = 2 * (2 * D * Q * I + Q * E * I)

F32 = mybir.dt.float32
BF16 = mybir.dt.bfloat16
I32 = mybir.dt.int32
U32 = mybir.dt.uint32
U16 = mybir.dt.uint16
U8 = mybir.dt.uint8
FP8X4 = mybir.dt.float8_e4m3fn_x4
ALU = mybir.AluOpType
ACT = mybir.ActivationFunctionType
AXIS_X = mybir.AxisListType.X

P = 128
PACK = 4
BANK = 512
QUADRANT = 32
E_TILES = E // P
T_BLOCKS = T // P
I_BLOCKS = I // P
ON_GPSIMD = 2
TINY = 1e-30

BANKS_A = (0, 1)
BANKS_B = (2, 3)
BANKS_FADE = (4, 5)
BANK_SIZE = 6
BANK_TURN = 7


def tile_attend_bagreement_v_kernel(
    tc, query, query2, keys_words, keys_scales, size, qs, grows, old, fade, offs, out
):
    nc = tc.nc
    with ExitStack() as ctx:
        sb = ctx.enter_context(tc.tile_pool(name="sb", bufs=1))
        ps = ctx.enter_context(tc.psum_pool(name="ps", bufs=1))

        def sbuf(shape, dtype, name, tag=None):
            return sb.tile(shape, dtype, name=name, tag=tag or name, align_bytes=64)

        def psum(bank, name):
            return ps.tile([P, BANK], F32, name=name, tag=f"bank{bank}")

        def half_of(h, width):
            return slice(h * width // 2, (h + 1) * width // 2)

        def block(n):
            return slice(n * P, (n + 1) * P)

        def load_k_first(src, name):
            raw = sbuf([P, PACK, src.shape[1]], F32, name)
            nc.sync.dma_start(raw[:], src.rearrange("(p j) c -> p j c", j=PACK))
            return raw

        def load_old(c):
            rows_of_old = sbuf([P, T], F32, f"old{c}")
            nc.sync.dma_start(rows_of_old[:], old[block(c), :])
            return rows_of_old

        offsets = sb.tile([P, I // 16], U16, name="offsets")
        nc.sync.dma_start(offsets[:], offs)
        qa_raw = load_k_first(query, "qa_raw")

        key_bytes = sbuf([P, T], U8, "key_bytes")
        for u in range(P // QUADRANT):
            four_rows = keys_scales[0, 4 * u : 4 * u + 4, :].bitcast(I32)
            nc.sync.dma_start(
                key_bytes[QUADRANT * u : QUADRANT * (u + 1), :].bitcast(I32),
                four_rows.unsqueeze(0).to_broadcast([QUADRANT // 4, 4, T // 4]),
            )

        rows = sbuf([P, P], F32, "rows")
        nc.gpsimd.memset(rows[:], 0.0)
        nc.sync.dma_start(rows[0:T_BLOCKS, :], fade.rearrange("o (b n) -> (o b) n", n=P))
        nc.sync.dma_start(rows[T_BLOCKS : T_BLOCKS + I_BLOCKS, :], size.rearrange("o (b n) -> (o b) n", n=P))

        key_words = sbuf([P, T], I32, "key_words")
        nc.sync.dma_start(key_words[:], keys_words[0].rearrange("p n t -> p (n t)").bitcast(I32))
        qb_raw = [load_k_first(query2[:, half_of(h, Q)], f"qb_raw{h}") for h in range(2)]
        qs_sb = sbuf([P, PACK], F32, "qs_sb")
        nc.sync.dma_start(qs_sb[:], qs.rearrange("(p r) o -> p (r o)", r=PACK))
        grows_raw = [load_k_first(grows[:, half_of(0, E)], "grows_raw0")]
        old_sb = [load_old(0)]
        grows_raw.append(load_k_first(grows[:, half_of(1, E)], "grows_raw1"))
        old_sb.extend(load_old(c) for c in range(1, E_TILES))

        ident = sbuf([P, P], F32, "ident")
        make_identity(nc, ident[:])

        placed = [sbuf([P, T], F32, f"placed{c}") for c in range(E_TILES)]
        for window in placed:
            nc.vector.memset(window[:], 0.0)

        def quantize(grouped, name, tag=None):
            words = grouped.shape[1] // PACK
            codes = sbuf([P, words], U32, name + "_codes", tag)
            scales = sbuf([P, words], U8, name + "_scales")
            nc.vector.quantize_mx(out=codes[:].bitcast(FP8X4), scales=scales[:], in_=grouped)
            return codes, scales

        def product(dst, lhs_codes, lhs_scales, rhs_codes, rhs_scales):
            nc.tensor.matmul_mx(
                out=dst,
                lhsT=lhs_codes.bitcast(FP8X4),
                lhsT_scale=lhs_scales,
                rhs=rhs_codes.bitcast(FP8X4),
                rhs_scale=rhs_scales,
                start=True,
                stop=True,
            )

        def scores(grouped, bank, name):
            codes, scales = quantize(grouped, name)
            pair = psum(bank, name + "_ps")[:].rearrange("p (k i) -> p k i", k=2)
            for k in range(2):
                product(pair[:, k, :], codes[:, block(k)], scales[:, block(k)], key_codes[:], key_scales[:])
            return pair

        def softmax_terms(pair, neg_max, total, h, name, tag=None):
            nc.vector.tensor_reduce(out=neg_max[:, half_of(h, PACK)], in_=pair, axis=AXIS_X, op=ALU.max, negate=True)
            terms = sbuf([P, 2, I], F32, name, tag)
            for k in range(2):
                r = 2 * h + k
                nc.scalar.activation(
                    terms[:, k, :], pair[:, k, :], ACT.Exp, bias=neg_max[:, r : r + 1], scale=1.0,
                    accum_out=total[:, r : r + 1],
                )
            return terms

        def interleave(engine_copy, grouped, raw):
            engine_copy(
                grouped.rearrange("p (c i j) -> p c j i", i=4, j=PACK),
                raw.rearrange("p j (c i) -> p c j i", i=4),
            )

        key_scales = sbuf([P, I], U8, "key_scales")
        nc.vector.tensor_copy(key_scales[:], key_bytes[:].indirect(offsets[:]))

        qa_dealt = qa_raw[:].rearrange("p j (s r) -> p s r j", r=PACK)
        qa_grouped = []
        for h, engine_copy in enumerate((nc.vector.tensor_copy, nc.scalar.copy)):
            grouped = sbuf([P, 2 * P * PACK], BF16, f"qa_grouped{h}")
            engine_copy(
                grouped[:].rearrange("p (r s j) -> p s r j", r=2, j=PACK), qa_dealt[:, :, half_of(h, PACK), :]
            )
            qa_grouped.append(grouped)

        key_codes = sbuf([P, I], U32, "key_codes")
        nc.vector.tensor_copy(key_codes[:], key_words[:].bitcast(U32).indirect(offsets[:]))

        turned_rows = psum(BANK_TURN, "turned_rows")
        nc.tensor.transpose(turned_rows[:, 0:P], rows[:], ident[:])
        columns = sbuf([P, T_BLOCKS + I_BLOCKS], F32, "columns")
        nc.scalar.copy(columns[:], turned_rows[:, 0 : T_BLOCKS + I_BLOCKS])

        def spread(dst, b):
            nc.tensor.transpose(dst, columns[:, b : b + 1].to_broadcast([P, P]), ident[:])

        fade_sb = sbuf([P, T], F32, "fade_sb")
        for h in range(2):
            fade_ps = psum(BANKS_FADE[h], f"fade_ps{h}")
            for m in range(T_BLOCKS // 2):
                spread(fade_ps[:, block(m)], h * T_BLOCKS // 2 + m)
            nc.scalar.copy(fade_sb[:, half_of(h, T)], fade_ps[:])
        size_ps = psum(BANK_SIZE, "size_ps")
        for m in range(I_BLOCKS):
            spread(size_ps[:, block(m)], T_BLOCKS + m)

        neg_max_a, sum_a, inv_sum_a, neg_max_b, sum_b = [
            sbuf([P, PACK], F32, name) for name in ("neg_max_a", "sum_a", "inv_sum_a", "neg_max_b", "sum_b")
        ]
        a_pairs = [scores(qa_grouped[h][:], BANKS_A[h], f"a{h}") for h in range(2)]

        qb_grouped = sbuf([P, Q * PACK], BF16, "qb_grouped")
        qb_view = qb_grouped[:].rearrange("p (r s j) -> p s r j", r=PACK, j=PACK)
        qb_dealt = [raw[:].rearrange("p j (s r) -> p s r j", r=PACK) for raw in qb_raw]
        nc.scalar.copy(qb_view[:, half_of(0, P)], qb_dealt[0])
        pa = [softmax_terms(a_pairs[h], neg_max_a, sum_a, h, f"pa{h}") for h in range(2)]
        nc.vector.tensor_copy(qb_view[:, half_of(1, P)], qb_dealt[1])
        b_pairs = [scores(qb_grouped[:, half_of(h, Q * PACK)], BANKS_B[h], f"b{h}") for h in range(2)]
        nc.vector.reciprocal(inv_sum_a[:], sum_a[:])

        grows_grouped = [sbuf([P, E // 2 * PACK], BF16, "grows_grouped0")]
        interleave(nc.scalar.copy, grows_grouped[0][:], grows_raw[0][:])
        pb = [
            softmax_terms(b_pairs[h], neg_max_b, sum_b, h, f"pb{h}", tag)
            for h, tag in enumerate(("grows_raw0", None))
        ]

        def fade_on_gpsimd(c, tag):
            result = sbuf([P, T], F32, f"faded{c}", tag)
            for h in range(2):
                cols = half_of(h, T)
                nc.gpsimd.tensor_tensor(result[:, cols], old_sb[c][:, cols], fade_sb[:, cols], ALU.mult)
            return result

        faded = [fade_on_gpsimd(0, "qb_grouped")]

        weighted = [sbuf([P, 2, I], F32, f"weighted{h}", f"b{h}_codes") for h in range(2)]
        for r in range(PACK):
            nc.vector.scalar_tensor_tensor(
                weighted[r // 2][:, r % 2, :], pa[r // 2][:, r % 2, :], qs_sb[:, r : r + 1], size_ps[:, 0:I],
                ALU.mult, ALU.mult,
            )
        dens = []
        for h in range(2):
            ratio = sbuf([P, 2], F32, f"ratio{h}")
            nc.vector.tensor_tensor(ratio[:], sum_b[:, half_of(h, PACK)], inv_sum_a[:, half_of(h, PACK)], ALU.mult)
            for k in range(2):
                den = sbuf([P, I], F32, f"den{2 * h + k}")
                nc.vector.scalar_tensor_tensor(
                    den[:], pa[h][:, k, :], ratio[:, k : k + 1], pb[h][:, k, :], ALU.mult, ALU.add
                )
                dens.append(den)
        nums = []
        for h in range(2):
            num = sbuf([P, 2, I], F32, f"num{h}")
            nc.vector.tensor_tensor(num[:], weighted[h][:], pb[h][:], ALU.mult)
            nums.append(num)

        def grows_columns(c):
            return grows_grouped[c // 2][:, half_of(c % 2, E // 2 * PACK)]

        grows_q = [quantize(grows_columns(0), "grows0")]

        wq = sbuf([P, PACK, I], F32, "wq")
        roots = []
        for step in range(PACK + 1):
            if step < PACK:
                root = sbuf([P, I], F32, f"root{step}")
                nc.scalar.activation(
                    root[:], dens[step][:], ACT.Abs_reciprocal_sqrt, bias=TINY, scale=sum_a[:, step : step + 1]
                )
                roots.append(root)
            if step > 0:
                r = step - 1
                inverse = sbuf([P, I], F32, f"inverse{r}")
                nc.scalar.activation(inverse[:], roots[r][:], ACT.Square)
                nc.vector.tensor_tensor(wq[:, r, :], inverse[:], nums[r // 2][:, r % 2, :], ALU.mult)

        last_root = f"root{PACK - 1}"
        grows_grouped.append(sbuf([P, E // 2 * PACK], BF16, "grows_grouped1", last_root))
        interleave(nc.scalar.copy, grows_grouped[1][:], grows_raw[1][:])

        wq_grouped = sbuf([P, I * PACK], BF16, "wq_grouped")
        wq_codes = sbuf([P, I], U32, "wq_codes")
        wq_scales = sbuf([P, I], U8, "wq_scales")
        for m in range(I_BLOCKS):
            interleave(nc.vector.tensor_copy, wq_grouped[:, half_of(m, I * PACK)], wq[:, :, block(m)])
        for m in range(I_BLOCKS):
            nc.vector.quantize_mx(
                out=wq_codes[:, block(m)].bitcast(FP8X4),
                scales=wq_scales[:, block(m)],
                in_=wq_grouped[:, half_of(m, I * PACK)],
            )

        for c in range(1, E_TILES):
            grows_q.append(quantize(grows_columns(c), f"grows{c}", "wq" if c == 1 else None))
        faded.append(fade_on_gpsimd(1, last_root))

        gv = []
        for c in range(E_TILES):
            gv_ps = psum(BANKS_A[c % 2], f"gv_ps{c}")
            product(gv_ps[:, 0:I], grows_q[c][0][:], grows_q[c][1][:], wq_codes[:], wq_scales[:])
            gv_sb = sbuf([P, I], F32, f"gv{c}")
            nc.scalar.copy(gv_sb[:], gv_ps[:, 0:I])
            gv.append(gv_sb)

        faded_banks = {2: (BANK_TURN, BANK_SIZE), 3: BANKS_FADE}
        faded_ps = {}
        for h, tag in enumerate(("wq_codes", None)):
            turned = sbuf([P, T_BLOCKS // 2, 2, P], F32, f"turned{h}", tag)
            for n in range(2):
                stage = psum(BANKS_B[n], f"stage{h}{n}")[:].rearrange("p (b c e) -> p b c e", b=2, c=2)
                first = h * T_BLOCKS // 2 + 2 * n
                for b in range(2):
                    for c in range(2):
                        nc.tensor.transpose(stage[:, b, c, :], old_sb[ON_GPSIMD + c][:, block(first + b)], ident[:])
                for b in range(2):
                    nc.scalar.activation(
                        turned[:, 2 * n + b, :, :], stage[:, b, :, :], ACT.Copy,
                        scale=columns[:, first + b : first + b + 1],
                    )
            for c in range(ON_GPSIMD, E_TILES):
                back = psum(faded_banks[c][h], f"faded_ps{c}{h}")
                for m in range(T_BLOCKS // 2):
                    nc.tensor.transpose(back[:, block(m)], turned[:, m, c - ON_GPSIMD, :], ident[:])
                faded_ps[(c, h)] = back

        for c in range(E_TILES):
            nc.vector.tensor_copy(placed[c][:].indirect(offsets[:]), gv[c][:])
        for c in range(E_TILES):
            result = sbuf([P, T], F32, f"result{c}")
            for h in range(2):
                cols = half_of(h, T)
                if c < ON_GPSIMD:
                    nc.gpsimd.tensor_tensor(result[:, cols], faded[c][:, cols], placed[c][:, cols], ALU.add)
                else:
                    nc.vector.tensor_tensor(result[:, cols], faded_ps[(c, h)][:], placed[c][:, cols], ALU.add)
                nc.sync.dma_start(out[block(c), cols], result[:, cols])
